import numpy as np, ml_dtypes
CORES = [25,29,33,37,73,77,185,189]
N = 8
import mx_ref
NC, KB = 256, 1
BF = ml_dtypes.bfloat16
def cut(t, i, w=512):
    return t[:, w * i:w * i + w]
def term(a, B):
    return np.stack([mx_ref.matmul(mx_ref.quantize(cut(a, i)), B) for i in range(4)], axis=2).reshape(128, -1)
def setup_inputs(rng):
    def f(*shape):
        return mx_ref.flush((rng.standard_normal(shape, dtype=np.float32) * np.exp2(rng.integers(-2, 3, shape[:-1] + (1,)))).astype(BF))
    return {"a": f(N, 128, 4 * 512), "b": f(N, 128, KB * 4 * NC)}
def setup_inputs_blocks(rng):
    d = setup_inputs(rng)
    for k in ("a", "b"): d[k] = mx_ref.spread(d[k], rng, 2)
    return d
def setup_inputs_wide(rng):
    d = setup_inputs(rng)
    for k in ("a", "b"): d[k] = mx_ref.flush((d[k].astype(np.float32) * np.exp2(rng.integers(-4, 5, (N, 1, 1))).astype(np.float32)).astype(BF))
    return d
def setup_inputs_lossless(rng):
    a = np.zeros((N, 128, 4 * 128, 4), np.float32)
    for r in range(N):
        k = rng.integers(0, 512, size=4 * 128)
        a[r, k // 4, np.arange(4 * 128), k % 4] = 1.0
    size = np.repeat(2.0 ** rng.integers(-4, 5, size=(1, 1, (KB * 4 * NC) // 4)), 4, axis=2)
    b = rng.integers(-1, 2, size=(N, 128, KB * 4 * NC)) * size
    return {"a": a.reshape(N, 128, 4 * 512).astype(BF), "b": b.astype(np.float32).astype(BF)}
def reference(a, b):
    y = np.zeros((N, 128, KB * 4 * NC), np.float32)
    for k in range(KB):
        y[:, :, 4 * NC * k:4 * NC * k + 4 * NC] = mx_ref.total([term(a[r], mx_ref.quantize(cut(b[r], k, 4 * NC))) for r in range(N)])
    return {"y": y}

from concourse.bass import DstId, RemoteDMATransfer
from concourse.mybir import dt, AluOpType, ActivationFunctionType

W = 128
CODES, PLANE = "float8_e4m3fn_x4", "uint8"
WORLD = range(256)

SCRATCH = {
    "abf": ("sbuf", [128, 2048], "bfloat16"),
    "bbf": ("sbuf", [128, 1024], "bfloat16"),
    "qa": ("sbuf", [128, 4 * W], CODES), "sa": ("sbuf", [128, 4 * W], PLANE),
    "qb": ("sbuf", [128, 2 * W], CODES), "sb": ("sbuf", [128, 2 * W], PLANE),
    "eye": ("sbuf", [128, 512], "bfloat16"),
    "qi": ("sbuf", [128, 4 * W], CODES), "si": ("sbuf", [128, 4 * W], PLANE),
    "tile": ("sbuf", [128, 1024], "bfloat16"),
    "qt": ("sbuf", [128, 2 * W], CODES), "st": ("sbuf", [128, 2 * W], PLANE),
    "hq": ("sbuf", [128, 4 * W], CODES), "hs": ("sbuf", [128, 4 * W], PLANE),
    "htile": ("sbuf", [128, 512], "bfloat16"),
    "qh": ("sbuf", [128, W], CODES), "sh": ("sbuf", [128, W], PLANE),
    "fq": ("sbuf", [128, 6 * W], CODES), "fs": ("sbuf", [128, 6 * W], PLANE),
    "yt": ("sbuf", [128, 1024], "float32"),
    "ps": ("psum", [128, 4096], "float32"),
}
SEMAPHORES = (["la0", "la1", "lb0", "lb1", "ones", "eye", "sent", "stored0", "stored1"]
              + ["qa%d" % i for i in range(4)] + ["qb0", "qb1"]
              + ["m%d" % i for i in range(8)] + ["c0", "c1", "qt0", "qt1"]
              + ["k%d" % i for i in range(4)]
              + ["h%d" % i for i in range(4)] + ["hm0", "hm1", "hc", "qh"]
              + ["pc%d" % i for i in range(6)] + ["ps%d" % i for i in range(6)]
              + ["d%d" % i for i in range(4)] + ["y0", "y1"])


def bits(mask):
    return bin(mask).count("1")


def near(topo, a, b):
    return topo.host(a) == topo.host(b) and topo.chip(a) == topo.chip(b)


def masks(topo, c):
    chip = next(d for d in WORLD if d != c and near(topo, c, d))
    away = next(d for d in WORLD if not near(topo, c, d) and topo.may_write(c, d))
    every, off = topo.mask(c, chip), topo.mask(c, away)
    return off & every, every & ~off


def plan(T, topo):
    cores = T.cores
    lead = cores[0]
    pairs = []
    for c in cores:
        if not any(c in p for p in pairs):
            pairs.append(sorted([d for d in cores if near(topo, c, d)], key=lambda d: topo.die(d) != topo.die(lead)))
    far = next(p for p in pairs if topo.host(p[0]) != topo.host(lead))
    even = next(p for p in pairs if topo.host(p[0]) == topo.host(lead) and not near(topo, p[0], lead)
                and not topo.same_plane(p[0], lead))
    odd = [p for p in pairs if p not in (far, even)]

    def on_die(at):
        return [c for c in WORLD if near(topo, c, at) and topo.die(c) == topo.die(at) and c not in cores]

    def helper(at, n):
        return [c for c in on_die(at) if all(topo.may_write(c, d) for d in cores)][n]
    hubs, relays, teams = [], [], []
    for s in range(2):
        o = 1 - s
        home, away = odd[o], odd[s]
        big, carry, small = helper(home[s], 0), helper(home[s], 1), away[s]
        e1, e2 = helper(even[s], 0), helper(even[s], 1)
        a, e, f = 2 * s, 2 * s + 1, 4 + s
        off, on = {}, {}
        for c in (big, carry, small, e1, e2, far[s]):
            off[c], on[c] = masks(topo, c)
        hubs.append((big, s, odd[0] + odd[1], a, [[(off[big], [even[s], even[o]]), (on[big], home)]]))
        hubs.append((small, s, odd[0] + odd[1], a, [[(off[small], [far[s]]), (on[small], [away[o]])]]))
        hubs.append((far[s], s, far, f, [[(off[far[s]], [carry]), (on[far[s]], [far[o]])], [(off[far[s]], [small])]]))
        hubs.append((e1, s, even, e, [[(off[e1], [far[s]])], [(off[e1], [odd[0][s], odd[0][o]])]]))
        hubs.append((e2, s, even, e, [[(off[e2], [odd[1][s], odd[1][o]]), (on[e2], even)]]))
        relays.append((far[s], a, 2, [(off[far[s]] | on[far[s]], [far[o]])]))
        relays.append((carry, f, 1, [(off[carry], [even[s], even[o]]), (on[carry], home)]))
        relays.append((small, f, 1, [(off[small] | on[small], [away[o]])]))
        teams.append([home[0], home[1], big, carry])
        teams.append([even[s], e1, e2, next(c for c in on_die(even[s]) if c not in (e1, e2))])
    teams.append([far[0], far[1], helper(far[0], 0), helper(far[1], 0)])
    return far, even, odd, hubs, relays, teams


def rank_program(g, core, T, topo):
    far, even, odd, hubs, relays, teams = plan(T, topo)
    team = next((t for t in teams if core in t), None)
    if team is None:
        return
    sem = T.sem
    rank = core in T.cores
    hub = next((h for h in hubs if h[0] == core), None)
    sent = [0]
    low, high = masks(topo, core)

    def ident(d):
        rid, pid = topo.addr(d, core)
        return DstId(rid=rid, pnc=pid)

    def call(transfers, out, src, name):
        g.remote_dma_fused([RemoteDMATransfer(dst_ids=[ident(d) for d in dsts], dma_engine_mask=mask,
                                              remote_sem=sem[name], srcs=[src], dsts=[out] * len(dsts), alu_op=0)
                            for mask, dsts in transfers], local_sem=sem.sent)
        sent[0] += sum(bits(mask) for mask, _ in transfers)

    def codes(transfers, oq, oc, q, c, n, name):
        call(transfers, oq[:, oc:oc + n].bitcast(dt.uint8), q[:, c:c + n].bitcast(dt.uint8), name)

    def scales(transfers, os, oc, s, c, n, name):
        call(transfers, os[:, oc:oc + n], s[:, c:c + n], name)

    def hop1(r, side):
        lo, hi = masks(topo, r)
        to = [h[0] for h in hubs if h[1] == side and r in h[2] and h[0] != r]
        on = [c for c in to if near(topo, c, r)]
        off = [c for c in to if c not in on]
        t = [(lo, off)] if off else []
        if on:
            t.append((hi if off else lo | hi, on))
        return t

    def slot(r):
        return next(h[2].index(r) for h in hubs if r in h[2])

    def landed(c, p):
        for transfers in [t for h in hubs if h[3] == p for t in h[4]] + [x[3] for x in relays if x[1] == p]:
            for mask, to in transfers:
                if c in to:
                    return bits(mask)
        return 0

    if rank:
        g.sync.dma_start(T.abf[:, 0:1024], T.a[:, 0:1024]).then_inc(sem.la0, 16)
        g.scalar.dma_start(T.bbf[:, 0:512], T.b[:, 0:512]).then_inc(sem.lb0, 16)
        g.sync.dma_start(T.abf[:, 1024:2048], T.a[:, 1024:2048]).then_inc(sem.la1, 16)
        g.scalar.dma_start(T.bbf[:, 512:1024], T.b[:, 512:1024]).then_inc(sem.lb1, 16)

    mine = team.index(core)
    part = slice(W * mine, W * mine + W)
    g.vector.memset(T.eye[:], 1.0).then_inc(sem.ones, 1)
    g.wait_ge(sem.ones, 1)
    g.affine_select(T.eye[:], T.eye[:], [[1, W], [-1, 4]], AluOpType.is_equal, 0.0, W * mine, -4).then_inc(sem.eye, 1)
    g.vector.wait_ge(sem.eye, 1)
    g.vector.quantize_mx(T.qi[:, part], T.si[:, part], T.eye[:, :]).then_inc(sem["k%d" % mine], 1)
    g.wait_ge(sem["k%d" % mine], 1)
    users = [c for c in team if c != core and (c in T.cores or any(h[0] == c for h in hubs))]
    codes([(low | high, users)], T.qi, W * mine, T.qi, W * mine, W, "k%d" % mine)
    scales([(low | high, users)], T.si, W * mine, T.si, W * mine, W, "k%d" % mine)

    def turn(q, s, c, bank, h, start, stop):
        return g.tensor.matmul_mx(T.ps[:, 512 * bank:512 * bank + 256], q[:, c:c + W], s[:, c:c + W],
                                  T.qi[:, 256 * h:256 * h + 256], T.si[:, 256 * h:256 * h + 256], start, stop)

    def move(vector, out, src, wait, done):
        if vector:
            g.vector.wait_ge(sem[wait], 1)
            g.vector.tensor_copy(out, src).then_inc(sem[done], 1)
        else:
            g.scalar.wait_ge(sem[wait], 1)
            g.scalar.activation(out, src, ActivationFunctionType.Copy).then_inc(sem[done], 1)

    def quantise_a(i):
        g.vector.quantize_mx(T.qa[:, W * i:W * i + W], T.sa[:, W * i:W * i + W],
                             T.abf[:, 512 * i:512 * i + 512]).then_inc(sem["qa%d" % i], 1)

    def quantise_b(side):
        g.vector.wait_ge(sem["lb%d" % side], 16)
        g.vector.quantize_mx(T.qb[:, W * side:W * side + W], T.sb[:, W * side:W * side + W],
                             T.bbf[:, 512 * side:512 * side + 512]).then_inc(sem["qb%d" % side], 1)

    def product(i, side):
        k = 4 * side + i
        g.tensor.matmul_mx(T.ps[:, 512 * k:512 * k + W], T.qa[:, W * i:W * i + W], T.sa[:, W * i:W * i + W],
                           T.qb[:, W * side:W * side + W], T.sb[:, W * side:W * side + W],
                           True, True).then_inc(sem["m%d" % k], 1)

    def move_term(i, side, vector):
        k = 4 * side + i
        move(vector, T.tile[:, 512 * side + i:512 * side + 512:4], T.ps[:, 512 * k:512 * k + W], "m%d" % k, "c%d" % side)

    def quantise_t(side):
        g.vector.wait_ge(sem["c%d" % side], 4)
        g.vector.quantize_mx(T.qt[:, W * side:W * side + W], T.st[:, W * side:W * side + W],
                             T.tile[:, 512 * side:512 * side + 512]).then_inc(sem["qt%d" % side], 1)

    if rank:
        g.vector.wait_ge(sem.la0, 16)
        quantise_a(0)
        quantise_a(1)
        quantise_b(0)
        g.vector.wait_ge(sem.la1, 16)
        quantise_a(2)
        quantise_a(3)
        quantise_b(1)
        for i in range(4):
            move_term(i, 0, i == 3)
        quantise_t(0)
        for i in range(4):
            move_term(i, 1, i % 2 == 1)
        quantise_t(1)
        for side in range(2):
            g.tensor.wait_ge(sem["qb%d" % side], 1)
            for i in range(4):
                if side == 0:
                    g.tensor.wait_ge(sem["qa%d" % i], 1)
                product(i, side)

        n = slot(core)
        for side in range(2):
            t = hop1(core, side)
            g.wait_ge(sem["qt%d" % side], 1)
            if t:
                codes(t, T.hq, W * n, T.qt, W * side, W, "h%d" % n)
                scales(t, T.hs, W * n, T.st, W * side, W, "h%d" % n)

    if rank or hub is not None:
        for k in range(4):
            g.tensor.wait_ge(sem["k%d" % k], 1 if k == mine else 2 * bits(low | high))
    if rank:
        for side in range(2):
            g.tensor.wait_ge(sem["c%d" % side], 4)

    if hub is not None:
        _, side, members, p, calls = hub

        def distance(c):
            return (c != core, not near(topo, c, core), topo.host(c) != topo.host(core), topo.die(c) != topo.die(core))
        order = sorted(members, key=distance)
        for n, c in enumerate(order):
            last = n == len(order) - 1
            if c == core:
                q, s, col = T.qt, T.st, W * side
                g.tensor.wait_ge(sem["qt%d" % side], 1)
            else:
                q, s, col = T.hq, T.hs, W * slot(c)
                m = next(mask for mask, to in hop1(c, side) if core in to)
                g.tensor.wait_ge(sem["h%d" % slot(c)], 2 * bits(m))
            for h in range(2):
                i = turn(q, s, col, h, h, n == 0, last)
                if last:
                    i.then_inc(sem["hm%d" % h], 1)
        move(True, T.htile[:, 0:256], T.ps[:, 0:256], "hm0", "hc")
        move(False, T.htile[:, 256:512], T.ps[:, 512:768], "hm1", "hc")
        g.vector.wait_ge(sem.hc, 2)
        g.vector.quantize_mx(T.qh[:, :], T.sh[:, :], T.htile[:, :]).then_inc(sem.qh, 1)
        g.wait_ge(sem.qh, 1)
        for t in calls:
            codes(t, T.fq, W * p, T.qh, 0, W, "pc%d" % p)
            scales(t, T.fs, W * p, T.sh, 0, W, "ps%d" % p)

    for c, p, n, t in relays:
        if c == core:
            for k in range(p, p + n):
                g.wait_ge(sem["pc%d" % k], landed(core, k))
            codes(t, T.fq, W * p, T.fq, W * p, W * n, "pc%d" % p)
            for k in range(p, p + n):
                g.wait_ge(sem["ps%d" % k], landed(core, k))
            scales(t, T.fs, W * p, T.fs, W * p, W * n, "ps%d" % p)

    if rank:
        for side in ([hub[1], 1 - hub[1]] if core in far else [0, 1]):
            a, e, f = 2 * side, 2 * side + 1, 4 + side
            parts = [f, a, e] if core in far else [e, a, f] if core in even else [a, e, f]
            for n, p in enumerate(parts):
                if hub is not None and hub[3] == p:
                    q, s, col = T.qh, T.sh, 0
                    g.tensor.wait_ge(sem.qh, 1)
                else:
                    q, s, col = T.fq, T.fs, W * p
                    if landed(core, p):
                        g.tensor.wait_ge(sem["pc%d" % p], landed(core, p))
                        g.tensor.wait_ge(sem["ps%d" % p], landed(core, p))
                last = n == len(parts) - 1
                for h in range(2):
                    i = turn(q, s, col, 2 + 2 * side + h, h, n == 0, last)
                    if last:
                        i.then_inc(sem["d%d" % (2 * side + h)], 1)
            for h in range(2):
                k = 2 * side + h
                move(h == 0, T.yt[:, 256 * k:256 * k + 256], T.ps[:, 512 * (2 + k):512 * (2 + k) + 256],
                     "d%d" % k, "y%d" % side)
            g.sync.wait_ge(sem["y%d" % side], 2)
            g.sync.dma_start(T.y[:, 512 * side:512 * side + 512],
                             T.yt[:, 512 * side:512 * side + 512]).then_inc(sem["stored%d" % side], 16)
        for side in range(2):
            g.sync.wait_ge(sem["stored%d" % side], 16)
    g.wait_ge(sem.sent, sent[0])
